import numpy as np, ml_dtypes
CORES = [0,1,2,3,4,5,6,7]
N = 8
T = 512
ROUTE = [[[4,5,3],[5,2,7],[7,0,5],[7,0,5],[3,2,7],[0,7,2],[3,6,5],[5,1,0],[1,3,2],[7,4,2],[0,3,5],[6,7,2],[6,1,7],[6,2,1],[3,6,5],[0,4,1],[5,7,4],[4,0,5],[7,0,3],[6,1,4],[0,4,3],[1,0,2],[5,4,6],[1,2,0],[3,4,0],[6,1,7],[3,2,0],[2,1,3],[4,6,2],[6,4,3],[6,0,2],[1,6,0],[0,6,7],[0,6,2],[5,6,2],[2,1,0],[7,6,5],[6,7,2],[1,7,3],[1,7,2],[6,1,2],[0,1,4],[0,1,7],[7,3,6],[2,5,7],[7,6,1],[5,6,7],[0,5,7],[5,3,2],[4,2,0],[1,3,7],[4,7,1],[7,5,4],[4,7,6],[7,4,6],[0,5,7],[1,5,7],[5,7,1],[3,5,1],[5,2,7],[0,5,2],[0,1,3],[3,0,6],[2,4,5],[5,1,3],[0,3,6],[2,3,7],[5,2,4],[5,4,3],[3,1,6],[2,0,3],[1,4,3],[2,1,5],[7,2,1],[7,4,5],[6,2,5],[1,0,3],[4,2,7],[4,3,0],[7,6,4],[0,2,4],[2,5,6],[6,0,1],[2,1,7],[5,7,2],[5,4,7],[4,5,2],[6,3,2],[3,2,1],[1,7,3],[3,5,1],[7,3,0],[1,7,5],[5,7,1],[3,0,6],[7,5,6],[5,4,6],[3,6,2],[6,1,4],[4,0,2],[0,6,4],[0,6,7],[7,0,6],[0,7,3],[0,6,4],[4,0,3],[2,6,3],[5,3,7],[7,2,3],[4,3,5],[2,0,7],[4,5,3],[4,6,2],[2,4,7],[0,7,4],[7,6,4],[5,2,1],[4,5,7],[2,3,0],[1,0,4],[2,5,4],[0,6,4],[3,4,5],[0,6,4],[7,3,2],[4,2,5],[3,4,7],[5,1,4],[7,2,1],[6,1,0],[6,7,3],[4,6,1],[5,4,2],[5,3,2],[0,3,6],[4,5,0],[5,2,7],[5,1,0],[5,2,6],[4,5,0],[6,4,0],[2,6,1],[1,7,4],[4,6,1],[5,2,4],[4,0,2],[2,7,5],[3,2,0],[1,2,5],[0,6,5],[3,0,5],[0,6,7],[0,7,4],[4,3,0],[1,2,7],[2,7,1],[5,0,6],[7,2,5],[7,6,1],[1,3,6],[5,6,7],[5,6,7],[0,5,1],[4,2,5],[3,4,2],[1,3,4],[6,7,5],[0,7,1],[4,6,1],[2,5,4],[4,5,2],[5,7,4],[1,7,4],[4,1,2],[1,6,0],[2,3,7],[3,4,0],[0,7,1],[0,5,3],[7,2,4],[2,5,7],[5,6,0],[1,3,6],[5,1,4],[7,0,6],[1,6,2],[4,7,3],[7,2,6],[5,7,0],[0,2,7],[3,4,5],[5,6,4],[2,1,6],[4,0,7],[4,5,0],[7,2,4],[3,2,6],[5,0,6],[0,5,6],[3,7,2],[0,5,6],[4,2,0],[3,6,2],[0,1,3],[1,5,4],[3,5,7],[4,3,6],[3,5,4],[2,3,5],[2,3,5],[6,1,0],[4,2,5],[7,3,6],[0,5,6],[0,3,1],[7,4,2],[1,7,2],[2,6,4],[6,4,3],[5,7,4],[3,1,5],[3,5,0],[5,3,2],[2,7,5],[1,0,7],[4,5,1],[1,6,4],[2,0,6],[3,5,4],[0,7,5],[1,3,2],[5,1,3],[1,0,2],[2,1,7],[2,0,7],[5,2,4],[3,0,1],[0,2,5],[3,2,6],[5,3,1],[6,7,4],[6,0,5],[5,2,6],[0,3,6],[7,2,1],[1,6,5],[3,6,4],[0,4,7],[2,5,3],[2,3,7],[3,5,1],[2,7,5],[5,1,0],[7,3,4],[3,1,6],[6,4,7],[2,5,7],[7,2,6],[2,5,1],[0,2,3],[0,6,4],[4,6,5],[1,3,4],[0,5,4],[2,3,6],[1,4,6],[1,7,2],[1,3,5],[1,0,4],[2,4,7],[6,5,7],[3,4,7],[5,7,6],[7,0,1],[0,5,2],[6,4,1],[3,6,4],[1,6,7],[2,5,1],[2,1,0],[6,1,0],[0,5,1],[1,3,4],[0,1,4],[3,4,7],[4,5,7],[5,4,3],[2,4,1],[6,2,7],[1,4,6],[6,2,4],[7,5,0],[0,6,7],[3,4,6],[7,6,4],[3,7,1],[5,3,0],[1,7,3],[6,5,7],[7,2,1],[7,6,3],[5,3,4],[7,1,4],[0,5,2],[1,0,3],[2,7,0],[6,4,3],[6,5,1],[3,1,6],[7,5,6],[5,1,7],[2,1,6],[4,1,0],[7,3,5],[3,6,4],[1,5,2],[2,4,6],[7,0,1],[7,3,4],[6,4,5],[5,0,7],[5,1,7],[2,1,7],[2,3,5],[4,7,0],[2,3,1],[1,4,3],[0,4,5],[7,0,4],[5,6,7],[1,3,7],[1,4,6],[2,1,4],[1,6,7],[3,6,0],[3,6,7],[3,6,5],[2,1,0],[6,7,2],[7,5,0],[6,7,5],[6,3,5],[1,3,7],[3,2,1],[4,7,6],[0,1,3],[1,6,5],[5,0,6],[4,6,5],[2,7,6],[7,0,3],[5,0,6],[3,6,2],[4,2,3],[4,0,7],[6,2,5],[7,5,1],[4,7,5],[4,2,5],[2,4,3],[0,6,7],[7,6,0],[6,2,1],[0,4,6],[5,2,1],[5,2,0],[5,7,3],[1,0,2],[5,2,6],[5,1,0],[6,7,0],[5,4,7],[1,7,6],[2,0,4],[3,5,7],[6,0,4],[3,7,1],[7,2,3],[1,6,0],[4,6,3],[0,2,4],[1,3,4],[4,3,0],[7,0,1],[7,2,4],[4,2,7],[4,7,0],[6,4,2],[1,0,7],[7,3,4],[2,0,4],[1,4,0],[6,7,4],[2,4,0],[7,5,2],[4,7,2],[7,0,3],[4,7,1],[7,1,4],[4,0,6],[6,1,5],[7,0,5],[6,4,3],[4,2,1],[2,6,7],[6,7,4],[1,2,6],[0,5,6],[7,5,0],[1,0,4],[6,7,5],[2,5,1],[7,0,4],[3,2,7],[1,4,7],[5,4,0],[6,1,3],[4,6,2],[3,7,0],[6,3,5],[5,3,2],[7,4,3],[4,1,2],[5,3,0],[4,2,5],[5,0,1],[4,2,6],[6,4,0],[0,4,7],[6,3,4],[2,6,5],[5,2,6],[1,6,7],[5,0,4],[6,0,2],[2,3,7],[0,5,2],[1,0,3],[7,4,0],[4,3,1],[2,7,4],[6,2,0],[3,7,6],[2,6,0],[4,5,6],[1,5,0],[0,7,5],[5,3,2],[3,5,4],[3,2,1],[1,4,6],[6,2,1],[6,2,5],[1,0,3],[4,2,6],[2,4,5],[2,0,3],[7,5,6],[5,2,0],[7,3,4],[5,6,1],[7,5,0],[2,5,6],[6,0,4],[4,3,7],[0,7,5],[5,3,7],[4,5,6],[7,6,5],[1,0,2],[1,7,0],[4,3,0],[6,5,2],[4,2,7],[2,1,5],[2,5,4],[0,2,4],[7,1,5],[5,6,1],[6,2,5],[5,3,6],[7,3,1],[7,2,6],[6,1,2],[1,4,6],[7,6,1],[2,4,7],[7,3,0],[0,5,4],[0,3,6],[5,6,2],[2,3,7],[0,3,7],[6,1,2],[2,7,3],[3,2,1],[0,1,6],[2,6,5],[5,2,0],[0,7,3],[0,2,1],[2,0,4],[7,2,4],[5,2,0],[2,0,1],[7,5,6],[5,1,3],[3,5,0],[2,7,1],[5,7,4],[4,3,5],[7,4,1]],[[1,0,3],[4,3,7],[3,7,4],[5,7,4],[0,5,1],[5,2,7],[4,0,2],[4,2,5],[3,4,6],[0,3,2],[5,1,2],[4,3,2],[5,2,7],[7,3,5],[1,5,7],[0,1,2],[7,6,1],[4,2,3],[5,7,4],[3,2,7],[4,5,1],[5,6,0],[3,2,0],[5,7,4],[1,3,5],[3,1,5],[1,7,3],[3,4,5],[1,7,3],[1,3,2],[4,2,5],[5,3,2],[6,0,4],[5,1,0],[1,5,0],[7,1,3],[2,3,0],[5,7,0],[5,2,0],[1,7,5],[1,3,7],[0,2,6],[3,6,2],[3,0,6],[0,2,4],[6,3,5],[3,6,4],[4,6,3],[3,2,6],[3,2,6],[1,2,4],[6,7,4],[5,3,6],[5,1,4],[5,4,2],[1,7,3],[5,3,6],[3,5,1],[7,6,2],[3,4,0],[3,4,7],[3,7,1],[6,1,3],[0,7,5],[3,2,6],[4,2,7],[4,0,5],[3,4,7],[4,0,2],[3,5,7],[4,3,1],[1,5,0],[4,2,7],[0,1,6],[5,6,0],[7,5,0],[0,4,3],[0,3,1],[3,0,7],[0,7,6],[6,0,4],[3,0,2],[4,6,5],[6,4,0],[2,0,1],[1,0,3],[1,7,4],[1,0,3],[1,7,6],[1,6,2],[1,7,0],[0,6,7],[6,5,4],[2,1,5],[3,5,6],[6,4,3],[4,3,1],[6,1,2],[1,3,7],[1,3,5],[0,4,6],[6,2,4],[1,4,5],[5,2,6],[5,4,1],[2,1,4],[3,0,7],[6,3,4],[3,5,6],[2,7,4],[6,2,0],[4,0,3],[5,2,4],[5,2,6],[1,3,2],[1,4,0],[5,4,3],[0,3,6],[2,7,1],[5,3,0],[6,1,5],[6,2,3],[7,1,0],[3,0,7],[3,7,2],[3,6,4],[1,3,2],[7,4,2],[4,6,5],[3,6,7],[4,1,3],[4,3,2],[5,7,6],[7,4,3],[1,5,4],[7,2,3],[4,5,0],[0,2,4],[2,7,3],[7,5,4],[2,6,3],[6,2,5],[0,5,1],[3,0,6],[4,2,0],[0,5,1],[3,5,1],[1,4,5],[6,5,7],[2,1,4],[3,0,5],[6,5,7],[6,5,2],[3,0,1],[1,3,5],[5,3,1],[2,0,7],[1,2,7],[7,5,0],[7,0,5],[3,6,0],[7,0,1],[6,2,7],[0,4,5],[3,6,5],[7,6,2],[2,3,6],[1,0,5],[6,1,7],[0,7,3],[5,1,3],[4,6,3],[4,3,5],[5,2,4],[4,2,6],[1,7,3],[4,0,5],[5,7,6],[4,2,0],[6,3,5],[0,6,1],[1,5,0],[6,5,4],[6,0,3],[4,3,5],[2,6,3],[5,0,1],[0,6,2],[7,4,6],[3,1,4],[5,0,4],[5,3,1],[1,6,7],[6,3,0],[2,4,7],[1,2,3],[7,3,1],[2,7,5],[4,2,6],[2,6,4],[3,1,7],[5,0,7],[2,6,5],[1,6,7],[0,2,3],[1,6,5],[1,2,7],[6,3,0],[3,7,1],[0,6,5],[1,3,6],[7,1,6],[3,0,6],[2,7,1],[0,2,5],[2,4,7],[4,6,3],[6,4,5],[5,3,4],[3,1,2],[5,0,4],[5,3,4],[0,6,3],[1,2,4],[7,1,2],[0,1,5],[5,6,1],[6,1,0],[2,1,0],[0,7,5],[6,4,2],[1,0,6],[6,7,2],[3,1,5],[1,7,0],[4,6,5],[6,1,2],[1,0,2],[2,1,5],[0,4,6],[7,6,4],[3,6,7],[7,2,1],[2,4,5],[5,3,4],[5,1,4],[3,4,5],[0,3,2],[2,5,0],[6,5,7],[3,0,7],[4,6,1],[4,1,5],[3,2,5],[7,4,3],[5,1,7],[0,7,2],[4,2,0],[3,6,2],[5,0,2],[2,1,7],[2,3,1],[4,2,5],[2,7,4],[5,0,4],[1,5,2],[2,6,5],[5,3,4],[6,1,2],[4,7,0],[4,5,3],[1,2,4],[2,6,1],[1,7,3],[0,4,7],[0,4,2],[7,0,4],[1,0,2],[5,2,6],[6,2,4],[6,4,1],[4,6,0],[6,7,5],[3,5,0],[3,6,2],[2,7,6],[7,1,6],[0,6,1],[1,6,3],[7,0,4],[7,1,4],[5,6,3],[2,3,6],[7,5,6],[2,7,1],[2,1,5],[1,7,5],[6,7,5],[1,4,0],[1,0,4],[5,4,6],[6,4,2],[4,5,2],[7,5,0],[1,7,0],[2,1,0],[2,7,3],[0,4,6],[0,4,3],[5,2,3],[3,1,5],[4,3,2],[2,0,5],[3,1,5],[7,2,4],[6,3,0],[3,7,0],[0,6,1],[1,4,5],[1,0,6],[0,6,7],[1,6,0],[2,0,7],[7,6,1],[7,6,4],[1,6,5],[0,2,4],[5,7,6],[7,4,3],[3,2,1],[3,7,6],[0,6,5],[7,4,6],[3,4,6],[0,1,3],[1,4,5],[0,4,6],[1,0,5],[1,7,0],[3,5,1],[5,0,2],[4,6,7],[0,1,5],[3,1,4],[0,2,7],[4,0,6],[7,4,3],[2,5,4],[6,2,4],[6,2,7],[1,0,3],[2,6,5],[6,3,7],[6,4,7],[2,4,1],[2,6,7],[5,1,7],[4,0,2],[0,3,7],[1,2,0],[5,6,2],[2,7,5],[0,1,6],[0,2,6],[5,0,7],[0,4,6],[3,4,7],[6,5,0],[6,5,1],[7,0,1],[2,4,0],[4,3,6],[1,6,7],[3,1,0],[2,4,6],[0,5,1],[4,7,5],[0,5,7],[3,0,7],[1,2,0],[5,0,4],[7,4,3],[6,5,0],[4,5,3],[6,2,4],[6,4,3],[5,0,2],[5,2,7],[3,5,6],[1,2,0],[7,6,0],[0,2,1],[5,4,0],[4,5,7],[7,1,5],[0,4,1],[2,4,1],[6,0,3],[1,6,2],[6,0,5],[7,2,0],[2,0,5],[7,2,6],[6,4,5],[5,4,7],[0,4,1],[6,2,7],[4,1,3],[0,4,3],[3,1,2],[3,2,1],[5,1,0],[6,3,4],[2,4,5],[2,3,1],[0,3,4],[0,5,1],[0,4,7],[4,5,1],[1,4,2],[7,0,1],[5,1,2],[1,2,3],[2,4,5],[2,5,1],[4,6,2],[2,3,4],[2,0,7],[6,1,2],[3,4,7],[5,2,1],[6,5,7],[1,0,6],[5,6,4],[4,6,2],[2,3,1],[1,3,2],[0,7,4],[0,1,4],[2,1,4],[6,5,1],[2,1,7],[0,2,1],[0,3,7],[7,2,5],[2,0,6],[2,4,7],[4,7,2],[6,3,4],[1,0,4],[7,1,4],[2,6,0],[1,4,3],[1,5,3],[0,4,2],[2,6,5],[1,6,4],[1,3,6],[2,3,4],[6,1,7],[2,0,6],[3,5,6],[0,2,5],[7,5,1],[2,0,7],[4,2,7],[1,3,6],[7,5,0],[2,5,1],[0,3,4],[2,6,1],[2,5,1],[4,6,1],[4,0,1],[3,2,4],[4,0,7],[6,7,0],[7,6,3],[4,0,1],[6,4,7],[5,7,2],[3,1,7],[7,0,3],[6,0,4],[2,1,3],[3,1,5],[2,1,5],[2,5,6],[7,2,0],[4,2,1],[0,3,6],[2,3,1],[6,4,5],[5,7,3],[0,1,4],[3,0,7],[7,1,2],[1,2,6],[3,7,1],[6,3,2],[2,7,6],[0,3,1],[6,1,2],[7,4,5],[2,7,0],[1,3,0],[0,2,6],[4,5,2],[6,4,7],[7,1,0],[5,0,3],[3,6,7]],[[0,7,1],[1,3,5],[2,0,1],[7,2,4],[0,1,5],[1,6,5],[1,7,2],[2,1,7],[0,7,2],[7,4,1],[7,1,6],[1,0,4],[3,5,1],[7,2,6],[3,2,7],[5,4,3],[2,6,0],[4,3,1],[2,5,1],[3,0,6],[4,7,0],[3,6,1],[5,3,1],[7,4,0],[6,4,0],[2,7,1],[2,1,5],[0,4,5],[7,4,5],[2,0,1],[2,7,3],[1,5,3],[3,1,0],[3,0,2],[7,3,1],[2,3,4],[3,6,0],[3,0,1],[6,1,5],[1,5,6],[3,5,7],[4,5,0],[1,6,5],[5,7,0],[7,3,2],[7,5,3],[2,6,4],[6,0,3],[1,7,0],[2,6,3],[1,2,4],[1,7,5],[3,2,6],[1,7,6],[1,5,0],[0,7,3],[3,0,7],[5,4,1],[1,5,4],[5,6,7],[2,6,7],[3,6,0],[1,6,5],[4,3,6],[1,6,2],[2,0,4],[3,7,6],[6,0,1],[6,0,3],[2,3,6],[7,4,6],[3,5,0],[1,5,7],[6,1,0],[0,3,1],[4,0,3],[3,2,5],[5,1,2],[0,6,1],[3,0,6],[0,2,7],[7,2,3],[1,5,0],[4,3,0],[1,7,0],[0,5,7],[6,2,5],[1,6,5],[5,1,3],[6,3,2],[4,7,2],[5,6,4],[0,5,4],[5,2,4],[2,6,0],[5,0,4],[3,7,4],[4,0,5],[3,4,6],[7,4,6],[1,5,0],[6,4,0],[5,0,3],[1,4,0],[4,2,5],[1,7,0],[6,0,5],[0,4,5],[0,6,3],[6,7,3],[6,0,4],[3,2,1],[1,6,7],[0,1,3],[1,0,6],[1,3,2],[4,7,1],[5,1,2],[2,4,3],[1,4,2],[7,0,6],[6,0,5],[4,5,7],[1,7,5],[5,3,0],[6,7,2],[4,7,0],[5,0,1],[4,6,5],[1,0,3],[4,6,1],[1,6,7],[6,4,3],[1,4,6],[7,0,5],[0,3,5],[4,1,5],[0,3,4],[0,7,6],[5,4,1],[5,6,4],[6,3,1],[1,4,3],[2,3,4],[1,4,0],[3,5,4],[1,2,7],[1,7,3],[2,4,5],[0,3,4],[4,3,1],[5,0,3],[1,4,2],[5,2,4],[7,0,4],[7,4,1],[6,4,2],[2,0,3],[1,6,0],[5,3,6],[7,3,0],[5,1,0],[1,0,7],[5,0,2],[1,2,4],[3,6,7],[0,4,3],[1,3,5],[4,5,3],[6,2,5],[3,5,6],[0,3,4],[4,1,0],[1,0,3],[1,4,7],[6,1,5],[5,6,3],[6,2,7],[3,0,6],[6,7,0],[3,4,2],[6,5,2],[4,5,2],[5,3,6],[5,4,3],[5,3,7],[4,6,1],[6,3,0],[4,2,1],[0,6,3],[7,3,6],[6,7,1],[3,5,4],[3,4,6],[4,7,5],[7,2,6],[2,1,5],[1,0,6],[2,3,0],[6,3,5],[0,2,7],[1,7,6],[0,5,6],[6,4,2],[7,2,6],[2,0,5],[6,0,3],[5,1,3],[6,5,3],[3,6,0],[5,7,2],[2,6,5],[5,1,4],[3,2,5],[5,3,7],[2,1,0],[4,2,6],[1,7,5],[6,5,0],[2,4,3],[1,0,6],[4,0,6],[1,7,3],[3,5,2],[6,3,1],[0,2,7],[2,1,3],[0,1,5],[6,5,1],[7,6,2],[3,6,1],[0,5,7],[4,6,5],[3,7,0],[2,0,7],[7,3,4],[0,4,6],[7,0,6],[3,2,5],[6,1,0],[4,2,7],[1,6,4],[2,7,1],[2,5,0],[3,4,1],[5,1,6],[0,1,5],[0,1,4],[0,6,5],[6,1,5],[4,6,3],[0,1,5],[0,2,3],[3,5,1],[4,3,6],[3,6,0],[7,5,0],[2,3,7],[2,3,0],[3,7,1],[1,0,5],[7,2,4],[3,7,0],[5,6,4],[4,0,1],[4,2,6],[2,0,3],[2,1,3],[4,5,0],[1,3,0],[6,4,3],[1,2,6],[6,2,4],[3,7,6],[3,2,5],[7,6,1],[7,5,6],[7,6,4],[6,5,4],[0,7,2],[0,6,2],[2,6,0],[0,2,3],[6,2,3],[7,5,6],[3,7,6],[4,7,0],[4,7,3],[7,4,1],[6,2,5],[7,1,0],[2,6,0],[6,5,2],[7,2,6],[0,3,2],[5,3,6],[3,4,5],[2,3,7],[1,4,5],[4,2,6],[1,7,6],[1,7,0],[2,0,6],[7,2,3],[6,5,4],[0,2,4],[2,1,0],[1,4,7],[3,5,0],[5,4,7],[6,5,3],[3,6,0],[2,6,0],[7,5,1],[6,3,1],[0,7,2],[4,1,5],[3,6,1],[1,4,2],[7,5,6],[0,6,5],[6,1,5],[1,4,6],[6,4,7],[1,5,3],[6,2,3],[4,0,6],[0,6,3],[2,0,4],[2,7,1],[6,4,5],[3,1,0],[6,0,4],[2,5,4],[7,2,5],[2,6,0],[6,7,4],[2,5,0],[5,6,2],[7,0,5],[5,2,1],[7,3,4],[6,1,4],[3,7,4],[4,7,3],[0,1,3],[2,7,4],[4,3,2],[0,4,1],[5,1,6],[6,7,0],[0,2,7],[1,4,3],[3,1,2],[5,4,6],[3,0,6],[6,5,4],[3,4,1],[2,1,7],[4,6,2],[6,4,5],[7,1,5],[6,0,3],[1,4,5],[6,7,2],[3,2,6],[1,0,6],[1,3,2],[7,1,6],[6,1,3],[2,1,0],[4,1,6],[3,4,1],[0,4,3],[3,1,7],[6,0,3],[3,1,0],[5,1,6],[1,2,4],[1,4,5],[1,2,7],[4,7,6],[2,4,7],[2,6,0],[5,6,1],[0,4,2],[4,1,6],[4,7,1],[2,7,6],[1,7,6],[3,5,1],[3,0,5],[6,7,5],[0,3,2],[5,7,0],[6,7,4],[1,0,5],[4,1,7],[0,6,2],[6,5,2],[0,5,4],[3,0,4],[2,0,5],[0,4,5],[3,0,7],[4,6,0],[3,5,7],[6,3,7],[5,0,1],[1,6,4],[6,3,5],[4,1,3],[0,1,4],[0,6,3],[4,6,7],[0,6,1],[7,6,0],[2,4,7],[7,3,6],[4,7,1],[7,1,6],[3,2,6],[6,4,3],[2,1,0],[1,3,0],[2,4,1],[4,2,7],[1,2,4],[3,7,1],[2,5,7],[5,6,4],[5,2,6],[0,6,5],[0,2,1],[1,3,6],[7,0,1],[0,7,4],[0,5,2],[1,3,4],[4,0,1],[0,7,1],[4,5,7],[5,3,1],[5,1,0],[2,1,0],[5,4,3],[3,7,0],[4,6,3],[7,3,2],[5,6,4],[0,1,4],[3,5,6],[1,0,3],[1,6,2],[4,6,2],[2,7,4],[4,3,5],[1,0,2],[6,2,4],[7,3,2],[7,6,1],[5,6,1],[6,4,5],[0,2,5],[0,3,6],[1,7,4],[6,1,2],[4,1,6],[1,4,0],[4,2,0],[4,0,7],[4,5,2],[0,5,6],[2,4,5],[3,4,5],[0,3,4],[7,3,2],[6,2,4],[0,7,1],[3,4,7],[1,5,0],[5,4,3],[0,7,4],[3,4,7],[6,1,3],[5,6,7],[7,0,3],[2,0,1],[3,1,7],[4,7,6],[5,6,1],[7,3,4],[1,0,4],[5,4,1],[5,2,3],[5,3,4],[4,1,7],[7,6,0],[5,7,3],[0,7,2],[1,0,5],[2,1,6],[5,2,3],[5,3,4],[2,4,3],[0,1,4],[4,2,6],[1,0,6],[7,0,5],[3,2,4],[2,4,6],[3,7,5]],[[7,2,5],[6,3,7],[5,4,7],[2,5,4],[6,2,3],[4,3,0],[6,3,7],[3,2,4],[7,3,4],[6,5,4],[6,2,0],[1,2,3],[1,5,7],[5,0,3],[7,0,4],[2,1,5],[2,6,4],[6,3,4],[2,5,3],[7,4,6],[4,1,3],[5,1,7],[1,6,5],[5,1,4],[4,2,7],[0,7,6],[3,5,1],[6,2,0],[0,2,4],[3,4,5],[5,4,7],[5,4,6],[1,3,7],[6,4,3],[5,7,1],[6,0,5],[3,2,5],[7,2,5],[5,1,7],[4,0,2],[7,0,4],[3,1,4],[5,2,6],[4,2,6],[4,7,0],[3,1,2],[3,7,1],[7,2,3],[4,7,6],[1,0,6],[4,7,1],[2,1,4],[1,5,4],[5,4,0],[3,5,6],[6,7,1],[2,6,1],[2,0,5],[2,0,1],[5,0,6],[4,3,7],[1,7,4],[3,0,2],[4,0,5],[0,2,4],[3,2,5],[2,4,5],[4,0,2],[5,4,2],[5,7,2],[1,0,3],[6,1,7],[2,5,7],[0,4,1],[7,3,4],[6,4,1],[2,6,7],[3,2,1],[4,0,5],[7,1,0],[6,4,1],[0,2,6],[2,7,4],[1,5,4],[1,3,4],[3,0,7],[2,6,3],[6,4,3],[6,7,5],[1,4,5],[4,7,0],[6,0,5],[3,7,0],[4,6,3],[3,1,0],[7,1,4],[1,2,0],[5,4,6],[1,4,6],[3,6,2],[6,7,0],[0,5,6],[3,5,2],[3,1,2],[5,3,4],[0,5,4],[7,5,2],[7,5,0],[5,1,6],[0,7,1],[7,4,1],[5,3,0],[5,4,1],[2,1,7],[2,1,0],[6,7,1],[0,2,6],[0,4,6],[0,4,7],[1,3,4],[0,4,3],[6,4,7],[7,6,5],[3,0,5],[7,2,0],[6,5,4],[1,7,0],[3,5,4],[6,7,3],[4,6,1],[3,4,0],[7,4,5],[1,4,0],[7,0,3],[0,1,6],[3,7,5],[3,5,0],[7,5,0],[0,6,4],[2,7,0],[0,2,6],[3,5,7],[7,6,4],[1,0,6],[7,5,6],[3,4,0],[1,0,2],[4,7,3],[2,0,3],[6,0,5],[0,5,3],[4,7,5],[0,6,1],[0,4,3],[3,1,6],[5,1,6],[6,0,3],[4,3,5],[5,1,2],[6,4,3],[2,6,4],[7,3,6],[5,2,7],[5,0,3],[1,6,4],[6,3,5],[3,0,5],[4,5,2],[6,3,5],[0,3,1],[3,5,0],[5,1,3],[6,1,7],[1,7,0],[5,4,6],[0,6,5],[7,2,4],[5,7,3],[4,7,5],[3,5,6],[6,0,2],[7,2,3],[5,3,1],[0,1,6],[7,4,6],[0,7,6],[1,0,6],[5,0,6],[0,3,5],[6,7,4],[0,1,4],[1,7,6],[4,3,7],[3,7,2],[1,5,3],[3,6,5],[7,4,1],[0,1,4],[6,5,4],[4,1,3],[1,4,3],[4,0,5],[0,2,3],[3,0,4],[5,4,3],[7,4,6],[5,0,1],[4,7,1],[6,1,5],[4,6,1],[7,3,0],[1,7,4],[7,4,1],[5,1,7],[2,7,4],[4,5,2],[5,7,2],[6,2,0],[4,1,0],[4,6,0],[0,5,1],[0,2,4],[3,7,2],[1,4,3],[0,2,5],[2,5,6],[6,0,3],[6,7,5],[6,4,7],[7,5,6],[5,2,4],[5,7,4],[2,3,5],[6,2,7],[0,6,4],[5,3,1],[7,5,4],[1,4,6],[2,7,6],[5,2,7],[1,5,0],[0,3,6],[1,6,2],[5,0,2],[3,6,4],[2,4,1],[7,6,4],[7,5,6],[0,5,7],[1,5,6],[0,3,7],[6,2,0],[4,3,5],[1,3,7],[2,4,3],[6,7,2],[1,2,7],[3,6,4],[7,1,4],[0,2,5],[3,2,1],[1,5,4],[3,5,0],[5,2,7],[3,5,2],[4,7,0],[3,4,1],[6,7,0],[0,1,3],[3,7,1],[7,0,2],[3,0,7],[4,3,5],[4,3,0],[1,7,0],[6,3,4],[0,1,6],[5,1,4],[4,1,2],[0,2,3],[0,1,5],[6,3,5],[6,0,4],[1,0,5],[7,5,4],[0,1,7],[4,2,0],[7,6,1],[5,1,2],[0,5,6],[5,7,1],[7,6,1],[3,0,5],[2,3,7],[1,6,4],[2,7,1],[1,4,0],[1,3,0],[0,2,7],[4,2,0],[1,6,5],[5,4,7],[7,0,5],[4,5,7],[0,6,2],[0,7,6],[7,1,4],[3,0,4],[3,1,7],[3,1,2],[4,0,3],[0,5,1],[1,6,0],[5,7,3],[3,2,6],[6,3,4],[5,7,4],[2,0,6],[7,5,1],[5,1,4],[7,1,0],[5,3,7],[4,5,1],[3,6,0],[2,5,7],[2,5,7],[7,1,6],[6,4,7],[4,1,6],[3,5,1],[4,0,3],[5,4,0],[5,3,2],[7,0,4],[4,3,2],[2,1,5],[1,7,6],[2,7,5],[6,4,7],[1,0,2],[3,4,6],[5,7,4],[1,5,0],[1,3,4],[0,3,5],[3,2,5],[5,2,3],[0,2,1],[7,4,2],[3,7,1],[7,6,0],[7,5,2],[2,0,1],[4,2,1],[3,1,2],[5,2,4],[5,1,0],[3,5,0],[3,5,0],[7,4,5],[0,2,6],[5,4,6],[3,7,1],[7,1,0],[7,6,1],[2,0,4],[2,0,6],[7,1,3],[5,2,6],[7,0,5],[3,6,0],[5,7,2],[3,2,1],[5,2,6],[4,7,0],[5,2,3],[1,6,0],[4,0,5],[4,2,6],[2,6,5],[3,7,1],[4,6,3],[4,5,2],[1,3,7],[1,3,2],[3,2,1],[0,4,2],[2,0,6],[3,1,0],[3,0,6],[5,4,6],[6,2,7],[1,5,0],[5,7,0],[0,2,5],[4,5,1],[3,0,6],[1,2,6],[1,7,6],[1,7,0],[2,7,5],[2,1,7],[4,2,7],[3,0,2],[5,1,3],[2,3,6],[3,2,1],[7,6,5],[7,0,4],[7,0,3],[6,2,4],[0,2,7],[6,4,3],[1,4,2],[2,1,7],[1,3,6],[5,4,6],[5,2,6],[2,3,4],[5,1,7],[5,0,1],[2,5,0],[0,5,4],[6,0,3],[1,2,3],[1,4,5],[2,3,5],[7,5,4],[3,6,7],[4,2,6],[5,3,0],[5,7,4],[3,2,1],[2,1,6],[4,2,1],[0,5,2],[7,1,4],[7,2,1],[7,3,4],[6,3,7],[0,3,2],[4,2,1],[4,5,7],[1,2,0],[3,2,6],[2,3,1],[3,2,7],[5,1,0],[4,2,0],[7,4,3],[5,6,4],[4,6,1],[6,0,5],[5,3,0],[0,2,1],[0,5,4],[7,4,1],[2,4,1],[3,2,6],[3,0,7],[7,1,3],[3,7,5],[1,5,4],[2,5,4],[5,6,3],[7,0,5],[2,1,5],[2,1,7],[0,4,1],[5,1,2],[3,0,2],[6,4,3],[4,5,6],[7,3,1],[1,0,3],[5,4,6],[3,5,2],[3,6,0],[4,3,5],[1,7,5],[4,5,6],[0,6,1],[3,6,1],[1,3,7],[3,2,0],[4,5,7],[7,6,2],[1,7,5],[2,0,1],[1,5,2],[1,4,2],[4,3,5],[1,3,4],[6,4,0],[2,4,6],[1,7,3],[0,3,7],[6,0,3],[7,6,2],[7,3,0],[5,4,0],[1,2,6],[1,2,3],[3,6,2],[2,5,4],[4,6,2],[2,7,5],[1,5,4],[4,5,2],[0,4,2],[7,3,0],[1,6,2]],[[0,6,2],[7,3,5],[7,5,3],[4,1,3],[4,7,6],[2,3,5],[0,3,5],[1,3,0],[0,7,2],[1,6,0],[0,2,7],[0,3,4],[6,0,5],[7,1,3],[3,1,7],[0,5,7],[7,5,2],[6,1,5],[6,4,0],[2,3,5],[7,1,2],[5,3,2],[0,1,4],[2,6,4],[2,7,4],[2,0,7],[7,3,1],[5,7,1],[2,6,1],[5,0,7],[4,2,1],[7,5,1],[5,2,6],[3,7,2],[2,6,3],[5,2,6],[4,1,2],[0,1,4],[7,5,4],[0,3,7],[2,3,6],[5,7,6],[6,2,3],[3,6,7],[6,5,4],[6,0,4],[2,1,0],[4,6,7],[3,5,2],[6,0,2],[5,0,6],[1,4,2],[3,4,2],[1,5,3],[1,7,0],[1,0,6],[1,0,6],[6,0,3],[7,2,5],[1,7,6],[7,6,0],[4,6,2],[5,2,0],[4,6,2],[7,4,0],[4,0,1],[6,5,1],[1,3,7],[3,1,7],[1,3,5],[4,7,2],[6,7,0],[7,5,6],[1,2,5],[1,0,6],[7,2,0],[2,3,0],[3,1,6],[4,1,6],[4,7,0],[3,4,6],[7,2,0],[7,5,3],[0,3,6],[0,4,1],[4,3,1],[7,5,1],[0,4,2],[4,1,7],[2,4,1],[6,5,2],[1,3,0],[3,0,7],[3,6,0],[4,1,3],[0,7,2],[7,5,2],[1,7,4],[3,7,0],[4,2,7],[5,2,7],[6,4,0],[1,5,4],[7,2,3],[0,2,5],[3,4,6],[2,3,6],[5,7,2],[1,2,5],[1,6,7],[3,4,5],[0,5,2],[3,1,6],[4,3,1],[3,0,2],[5,1,3],[3,1,2],[2,6,7],[1,7,4],[1,7,4],[2,4,6],[1,5,4],[3,2,0],[7,5,4],[6,2,5],[7,0,3],[5,4,0],[2,5,4],[4,1,6],[3,4,5],[1,0,4],[7,4,3],[2,1,6],[5,2,4],[3,4,6],[2,7,5],[0,7,3],[2,4,3],[4,0,6],[2,1,3],[7,3,0],[3,0,1],[4,1,7],[4,3,2],[1,3,4],[4,1,3],[2,0,4],[7,3,2],[7,4,6],[0,1,5],[2,5,4],[4,3,2],[3,7,2],[5,2,0],[3,6,2],[1,0,3],[6,5,0],[4,3,2],[1,2,5],[2,4,5],[0,3,1],[5,6,7],[6,3,0],[3,5,2],[4,6,3],[4,7,6],[0,1,6],[4,0,5],[0,4,5],[2,4,0],[6,3,0],[4,6,1],[4,2,0],[6,4,1],[3,7,1],[3,0,5],[5,4,2],[5,0,4],[0,5,1],[2,0,5],[2,5,6],[0,7,1],[0,2,3],[0,4,3],[2,0,3],[5,1,6],[5,4,6],[0,6,7],[0,2,1],[0,1,7],[7,3,4],[2,3,4],[6,3,4],[4,6,0],[6,4,7],[7,4,2],[1,0,2],[6,1,4],[3,7,5],[6,5,2],[4,5,7],[4,1,0],[6,0,2],[1,4,7],[5,1,2],[2,1,0],[7,2,5],[1,7,5],[1,3,4],[6,4,7],[4,2,5],[1,2,0],[1,3,2],[2,5,3],[7,6,3],[0,7,2],[7,6,2],[3,7,1],[1,4,6],[3,0,5],[0,1,5],[6,7,0],[7,5,3],[2,0,3],[5,4,0],[7,0,1],[3,0,1],[3,2,4],[7,2,1],[0,2,7],[6,2,1],[7,3,1],[4,2,0],[0,5,1],[7,3,6],[1,7,6],[0,6,4],[6,7,4],[5,0,6],[4,2,6],[3,6,4],[7,3,2],[4,7,3],[1,6,2],[4,1,7],[5,0,6],[0,1,6],[3,1,4],[5,7,1],[0,4,3],[3,2,0],[7,6,1],[7,3,2],[4,2,1],[0,5,2],[6,2,5],[4,6,0],[3,7,6],[2,3,5],[5,3,6],[6,2,5],[4,5,6],[0,1,5],[5,3,4],[0,1,6],[7,2,5],[2,5,1],[0,4,7],[5,2,0],[5,6,2],[3,0,4],[4,1,0],[3,5,2],[1,0,3],[7,3,1],[7,0,6],[7,3,1],[5,4,7],[5,0,1],[7,3,1],[5,3,6],[5,0,3],[7,6,1],[5,7,0],[5,1,4],[6,3,7],[1,6,3],[5,6,2],[7,2,4],[7,6,4],[7,5,4],[7,4,3],[7,5,3],[0,1,6],[5,4,7],[5,1,3],[2,1,7],[5,4,3],[6,4,0],[1,4,2],[4,0,1],[6,1,4],[4,6,1],[7,5,0],[2,5,3],[7,5,3],[5,1,3],[4,0,5],[6,4,3],[0,5,7],[5,2,1],[3,4,5],[5,6,0],[2,5,7],[3,1,5],[3,7,6],[4,1,6],[5,4,0],[0,4,3],[0,6,2],[4,1,0],[4,1,5],[5,4,6],[5,3,2],[0,7,3],[4,1,7],[5,7,1],[1,5,2],[2,4,3],[4,0,2],[6,4,3],[6,1,3],[7,4,3],[4,5,0],[1,5,3],[7,1,3],[5,3,4],[7,4,2],[1,5,6],[4,3,6],[6,3,2],[3,6,7],[5,6,0],[6,7,4],[4,1,7],[1,2,0],[0,7,2],[1,0,5],[0,7,3],[0,6,2],[6,7,1],[4,7,0],[5,1,4],[5,4,0],[7,1,3],[5,3,6],[0,3,1],[4,2,7],[7,3,0],[2,0,7],[7,6,3],[4,2,7],[6,4,3],[3,0,4],[0,1,3],[2,7,0],[7,5,1],[4,3,5],[7,4,2],[1,7,6],[3,2,7],[7,6,4],[3,5,4],[1,0,4],[7,1,2],[4,2,3],[5,1,7],[1,4,2],[6,0,4],[2,5,4],[0,6,4],[7,3,2],[5,6,0],[2,0,6],[1,0,3],[4,2,0],[5,4,7],[0,4,3],[0,4,5],[7,2,4],[4,7,6],[2,3,7],[4,3,7],[5,1,6],[4,1,5],[6,4,0],[0,6,4],[0,2,7],[1,0,6],[0,7,5],[0,3,5],[7,4,5],[7,0,3],[6,1,7],[4,7,6],[3,1,0],[5,0,7],[6,2,0],[4,2,3],[7,3,5],[0,2,5],[4,2,5],[2,5,0],[1,5,6],[1,5,4],[0,1,6],[4,0,5],[2,1,5],[4,2,3],[0,1,5],[7,2,6],[3,5,0],[0,7,4],[2,0,6],[3,0,6],[7,4,6],[3,6,7],[2,0,4],[0,6,2],[7,6,4],[6,1,4],[0,3,6],[5,3,1],[2,0,4],[7,5,0],[3,7,6],[7,0,6],[0,4,1],[0,5,6],[0,1,6],[3,7,5],[0,6,3],[2,5,7],[7,4,6],[0,2,1],[4,7,0],[7,1,2],[4,2,6],[3,4,1],[5,4,7],[1,6,7],[2,3,7],[0,5,3],[4,1,6],[3,7,2],[6,1,7],[2,0,6],[0,4,7],[6,5,7],[1,7,6],[2,3,0],[3,2,1],[1,4,6],[5,0,4],[2,7,5],[6,7,2],[6,1,2],[7,4,1],[4,7,0],[1,3,5],[6,5,0],[5,1,7],[4,7,0],[4,6,0],[4,5,0],[0,1,3],[6,2,7],[3,0,6],[2,0,4],[4,7,1],[4,7,6],[0,4,3],[0,5,4],[6,1,4],[6,2,5],[0,7,6],[5,1,6],[2,7,0],[7,2,6],[4,1,3],[3,1,7],[7,6,2],[0,1,7],[1,3,0],[1,7,2],[3,0,5],[0,7,3],[6,7,5],[4,6,1],[5,4,0],[0,1,3],[0,7,2],[6,0,2],[6,4,3],[0,6,4],[3,1,2],[4,5,0],[7,0,2],[6,1,3],[7,3,2],[3,1,7],[1,7,4]],[[6,5,4],[5,4,1],[2,5,1],[1,4,6],[6,5,0],[2,5,7],[2,7,5],[7,3,4],[4,6,7],[2,7,4],[7,2,6],[6,1,7],[0,5,1],[7,2,4],[3,2,4],[5,2,4],[4,6,2],[4,0,5],[7,0,4],[3,1,6],[3,7,1],[5,6,4],[7,3,1],[7,4,6],[5,4,2],[2,7,6],[1,6,5],[0,1,7],[7,2,6],[7,4,1],[1,5,2],[6,1,4],[4,7,2],[7,3,4],[2,6,0],[0,5,7],[7,2,4],[7,4,5],[4,2,7],[3,5,7],[0,5,7],[6,0,1],[3,1,0],[3,1,0],[7,5,4],[7,0,2],[2,7,3],[6,0,1],[3,0,6],[6,1,0],[0,2,4],[6,4,3],[0,7,4],[1,0,6],[4,6,7],[4,6,3],[5,7,3],[0,2,3],[4,3,0],[1,0,5],[1,3,7],[4,3,6],[1,7,2],[6,7,0],[6,3,0],[5,0,4],[6,5,7],[4,2,0],[6,2,3],[6,5,1],[4,6,5],[6,7,0],[2,3,1],[1,0,5],[0,7,4],[0,4,6],[6,4,3],[6,4,0],[2,3,6],[7,1,2],[6,7,3],[1,0,6],[4,5,2],[5,2,3],[2,0,5],[3,7,2],[7,5,4],[6,1,2],[0,1,7],[7,2,4],[1,3,2],[7,6,1],[2,4,5],[2,7,1],[6,3,5],[6,5,2],[3,5,4],[7,2,4],[7,2,6],[5,2,6],[1,4,7],[1,2,4],[0,6,1],[7,3,0],[6,3,4],[1,6,5],[0,4,7],[4,6,2],[4,6,1],[2,4,1],[1,6,4],[6,1,2],[7,6,0],[0,1,2],[4,7,5],[4,0,5],[7,1,5],[3,6,0],[3,0,2],[2,1,5],[3,4,5],[7,6,0],[2,4,1],[7,6,1],[0,5,3],[6,2,4],[5,2,4],[6,4,1],[7,2,0],[0,1,6],[1,7,0],[1,0,4],[0,2,6],[2,6,0],[5,4,2],[6,5,7],[1,2,5],[0,3,2],[1,5,3],[3,5,0],[6,0,4],[5,2,0],[3,0,5],[4,6,5],[6,2,1],[7,6,3],[5,1,7],[0,7,6],[2,3,0],[3,0,2],[7,4,5],[2,1,5],[6,2,0],[4,1,0],[7,2,5],[2,1,3],[7,0,3],[0,1,6],[4,6,2],[2,0,5],[0,2,5],[5,2,6],[7,3,6],[6,7,5],[2,6,3],[3,6,1],[2,1,5],[0,7,4],[6,0,7],[6,2,7],[6,1,5],[2,4,3],[0,7,6],[2,7,4],[1,0,2],[2,0,6],[1,4,0],[1,2,0],[2,0,6],[6,1,3],[6,1,5],[6,5,7],[1,4,0],[7,4,6],[6,1,4],[1,6,5],[1,0,7],[5,2,1],[0,3,7],[5,6,4],[4,0,5],[0,5,2],[7,0,4],[2,0,7],[0,1,2],[4,1,5],[7,6,4],[7,2,3],[4,2,5],[7,0,1],[1,3,4],[1,4,0],[4,2,1],[1,3,2],[2,5,1],[3,6,4],[4,5,7],[0,4,2],[4,6,0],[4,1,3],[2,7,6],[1,4,7],[4,2,3],[3,5,2],[3,1,7],[5,3,2],[4,5,7],[1,2,6],[5,3,2],[0,7,6],[7,4,0],[6,5,1],[0,6,4],[5,7,4],[6,0,1],[3,4,6],[3,7,5],[6,3,7],[4,5,3],[2,5,1],[4,2,1],[1,0,2],[0,7,6],[1,0,3],[0,6,3],[4,5,1],[0,6,5],[1,2,3],[2,0,3],[2,5,1],[1,3,2],[2,4,3],[7,6,0],[2,0,6],[2,4,6],[7,1,0],[2,3,0],[1,0,4],[0,3,4],[5,3,4],[4,0,6],[1,0,3],[7,1,6],[1,6,7],[6,1,2],[4,6,1],[7,5,3],[1,3,7],[3,7,2],[0,4,7],[5,3,7],[2,7,0],[6,2,3],[2,4,7],[0,6,7],[2,4,0],[3,1,7],[0,2,3],[0,1,2],[3,1,2],[4,0,1],[0,2,4],[5,2,0],[6,7,2],[4,1,0],[5,6,1],[2,0,5],[5,7,0],[2,6,5],[2,5,3],[6,7,0],[5,3,7],[3,7,6],[3,7,4],[4,3,6],[5,1,4],[0,3,5],[7,5,3],[4,1,5],[2,0,3],[7,6,3],[2,6,7],[3,4,7],[7,5,3],[4,0,7],[3,6,7],[2,4,0],[3,5,0],[2,0,6],[0,2,5],[6,0,3],[7,1,2],[3,1,4],[1,5,0],[4,1,7],[1,0,4],[2,0,5],[7,5,3],[6,7,2],[0,5,7],[1,2,7],[3,5,4],[2,5,4],[1,4,7],[5,7,3],[1,6,4],[1,4,2],[3,0,6],[2,5,0],[2,7,3],[7,6,1],[4,2,6],[6,0,7],[7,1,6],[3,1,6],[5,7,3],[6,2,3],[7,2,4],[0,3,1],[1,0,4],[1,2,0],[2,4,7],[5,2,1],[3,5,2],[1,5,3],[3,4,5],[7,4,1],[0,5,3],[4,5,7],[5,3,1],[1,2,7],[6,0,7],[4,3,2],[2,4,0],[7,4,1],[6,5,3],[0,3,4],[2,6,0],[3,7,2],[4,6,5],[2,5,6],[7,3,6],[1,3,0],[5,6,4],[1,4,5],[6,4,2],[5,6,7],[5,4,0],[1,6,4],[7,0,1],[1,4,0],[1,2,7],[4,6,5],[3,4,6],[7,2,3],[6,0,1],[2,1,0],[0,3,1],[7,1,6],[1,4,2],[1,5,3],[5,3,1],[3,6,4],[1,7,4],[3,5,0],[5,6,0],[7,4,6],[3,0,2],[5,6,3],[6,2,3],[1,2,3],[7,0,4],[3,0,7],[1,5,6],[4,1,2],[2,7,1],[3,1,0],[0,4,7],[4,1,6],[3,4,2],[3,5,0],[3,6,2],[5,3,1],[6,5,7],[3,2,5],[1,0,7],[6,1,5],[1,5,2],[2,6,1],[0,7,3],[1,7,4],[1,5,3],[6,4,2],[1,4,2],[4,3,6],[6,1,5],[6,1,2],[5,6,3],[3,6,0],[1,0,4],[6,4,7],[2,7,0],[6,3,0],[0,3,7],[2,5,3],[7,4,5],[4,7,0],[0,2,3],[3,2,6],[5,4,7],[2,7,3],[5,1,6],[0,4,6],[5,4,3],[4,0,1],[2,4,3],[6,4,0],[3,2,1],[6,7,3],[6,1,4],[5,7,3],[4,1,7],[4,6,5],[6,1,2],[1,5,7],[0,4,6],[0,3,7],[6,0,4],[2,6,0],[5,7,2],[0,2,1],[1,3,5],[5,2,1],[3,0,2],[3,0,1],[7,0,3],[0,1,3],[1,4,3],[7,2,6],[0,2,7],[1,4,7],[6,4,5],[6,0,2],[3,5,6],[7,4,3],[3,0,6],[5,2,3],[1,4,0],[4,2,7],[3,5,6],[4,7,2],[4,1,6],[4,6,0],[0,4,1],[2,0,1],[6,2,0],[1,7,6],[4,7,0],[0,2,3],[5,4,2],[2,6,3],[2,6,4],[7,0,6],[3,7,0],[2,3,1],[2,0,1],[5,2,6],[5,3,2],[1,2,3],[1,4,0],[6,2,4],[1,6,2],[3,4,7],[7,2,3],[1,4,3],[5,0,3],[2,4,3],[7,4,5],[5,0,6],[5,0,7],[3,4,0],[6,4,3],[0,3,7],[0,2,4],[5,3,4],[5,4,6],[5,2,3],[2,1,5],[6,7,1],[5,1,7],[1,7,6],[4,0,5],[3,7,1],[6,2,5],[5,0,4],[7,6,2],[6,7,2],[6,2,4],[1,6,7],[2,1,7],[0,6,3],[0,7,3]],[[7,6,2],[0,6,4],[6,2,0],[3,1,6],[5,4,2],[5,0,3],[0,4,1],[0,2,5],[4,0,6],[1,4,6],[2,6,7],[3,1,5],[7,3,2],[4,6,2],[0,3,2],[1,2,5],[0,6,3],[2,7,5],[1,7,2],[3,7,0],[3,6,0],[7,1,2],[3,7,5],[1,2,3],[5,2,3],[4,0,6],[2,7,6],[2,7,4],[1,5,6],[5,7,2],[5,3,0],[2,5,7],[4,5,3],[3,1,7],[6,1,7],[0,3,5],[5,7,3],[2,6,0],[2,0,3],[5,6,3],[5,4,2],[3,1,4],[4,3,6],[2,7,5],[5,2,0],[2,3,4],[0,6,2],[7,1,3],[2,7,4],[0,7,2],[2,7,4],[6,1,7],[6,7,1],[1,2,4],[2,1,0],[2,5,3],[1,4,0],[4,1,0],[0,6,1],[5,0,2],[5,1,6],[5,4,1],[4,6,3],[7,2,0],[6,3,1],[5,1,4],[7,6,2],[1,3,0],[6,4,3],[6,3,1],[4,7,3],[7,4,6],[6,4,2],[2,3,1],[2,6,5],[0,3,4],[2,5,3],[5,7,1],[6,7,1],[2,1,0],[6,4,0],[1,6,5],[1,5,0],[2,0,7],[0,1,5],[7,6,5],[2,3,5],[3,0,4],[6,4,7],[7,6,0],[1,3,5],[7,2,6],[2,7,0],[0,2,1],[6,1,2],[7,6,3],[0,5,1],[5,6,2],[4,6,0],[0,1,6],[4,5,1],[6,5,4],[5,1,7],[4,7,3],[3,6,2],[5,6,0],[7,0,3],[1,3,4],[4,2,7],[7,4,3],[5,4,6],[6,7,4],[6,7,2],[4,3,6],[7,5,6],[1,0,6],[1,6,5],[3,6,7],[0,1,4],[1,2,5],[4,6,3],[6,5,0],[4,5,3],[3,1,4],[0,4,5],[0,2,6],[0,2,6],[7,5,0],[7,1,2],[5,4,6],[3,6,1],[2,3,6],[2,6,7],[5,1,0],[3,5,4],[7,6,3],[0,7,3],[6,2,4],[3,5,2],[4,6,2],[3,6,4],[5,2,0],[6,5,1],[0,6,1],[5,0,4],[0,3,2],[1,3,6],[3,6,0],[2,1,5],[0,6,7],[0,4,3],[2,4,3],[0,2,3],[6,0,1],[0,4,5],[6,3,4],[4,7,0],[3,7,0],[7,6,4],[4,6,1],[3,2,6],[0,7,3],[5,3,1],[1,3,5],[5,2,0],[3,2,7],[0,2,4],[5,0,3],[3,6,0],[7,3,2],[0,2,3],[3,2,1],[7,2,4],[5,1,3],[4,1,7],[0,2,7],[2,5,4],[1,6,7],[6,1,5],[0,1,3],[6,2,5],[3,5,0],[6,1,4],[7,3,4],[1,5,0],[5,4,6],[0,3,5],[7,6,2],[1,5,2],[4,1,6],[4,7,1],[5,4,7],[0,3,2],[7,3,6],[1,3,7],[3,4,7],[0,6,2],[7,2,0],[3,5,6],[0,1,7],[1,0,2],[0,5,1],[4,5,3],[1,5,0],[2,1,7],[5,7,6],[5,6,7],[0,5,2],[1,0,4],[3,7,6],[0,3,7],[5,0,3],[0,2,6],[2,7,5],[0,1,5],[2,1,3],[6,1,0],[5,2,0],[6,1,2],[6,2,5],[1,5,3],[4,1,0],[0,3,5],[3,0,6],[3,5,6],[1,5,4],[3,4,0],[3,0,4],[6,4,0],[1,6,5],[3,2,0],[4,2,5],[1,4,7],[0,6,2],[3,4,0],[5,6,2],[1,4,6],[3,2,6],[0,2,5],[5,6,3],[3,1,2],[2,0,5],[5,1,6],[2,1,6],[5,3,1],[3,2,6],[6,2,1],[1,5,0],[1,4,5],[6,7,4],[2,3,6],[1,6,3],[1,3,2],[6,5,4],[2,4,6],[0,1,2],[7,5,0],[4,1,3],[5,7,3],[7,2,4],[6,3,7],[0,5,2],[5,6,2],[3,7,0],[0,1,5],[1,3,6],[6,7,4],[2,7,3],[2,0,7],[6,5,0],[3,6,0],[1,2,4],[0,5,2],[3,5,2],[7,3,2],[4,1,2],[7,6,3],[3,5,0],[1,0,2],[3,0,4],[0,2,5],[6,2,0],[3,7,4],[0,4,7],[5,0,4],[4,3,6],[7,3,0],[1,3,4],[6,0,4],[6,3,7],[0,6,2],[1,5,6],[0,2,4],[1,4,0],[2,5,6],[6,3,7],[7,1,3],[6,5,3],[4,7,2],[6,7,5],[3,1,7],[0,6,3],[7,4,0],[3,1,5],[1,6,3],[6,5,0],[7,2,1],[6,5,3],[5,2,0],[3,2,1],[2,7,0],[3,6,4],[6,4,2],[5,2,6],[6,1,7],[3,2,4],[2,3,0],[4,3,1],[2,7,0],[2,5,4],[1,3,0],[5,3,2],[5,1,2],[0,2,1],[0,1,6],[0,6,3],[5,7,4],[6,5,7],[3,5,0],[4,5,1],[3,7,4],[2,0,7],[6,4,7],[7,3,5],[0,3,2],[0,1,2],[2,0,4],[3,2,4],[5,4,7],[3,0,1],[4,2,6],[4,5,0],[6,3,5],[5,7,1],[0,3,6],[4,3,0],[6,7,1],[3,6,0],[5,1,2],[6,2,7],[0,3,2],[1,0,2],[3,4,0],[5,2,0],[1,4,6],[6,5,3],[1,6,2],[3,7,6],[1,6,7],[1,7,3],[7,4,3],[0,7,5],[2,1,0],[3,6,2],[4,1,0],[5,4,1],[2,5,6],[7,0,1],[1,7,6],[5,1,0],[1,4,6],[7,6,0],[4,7,1],[6,2,0],[6,2,3],[2,1,3],[3,4,2],[3,4,1],[5,0,6],[3,7,0],[7,1,6],[3,0,7],[6,1,2],[7,3,0],[7,2,3],[4,5,6],[0,3,6],[3,0,4],[6,3,4],[6,7,1],[1,3,2],[4,6,5],[7,2,5],[5,3,6],[0,6,2],[3,6,7],[4,7,3],[2,6,4],[3,5,7],[5,3,6],[7,4,2],[0,6,3],[1,5,6],[6,1,4],[3,6,0],[5,2,0],[4,1,6],[3,5,4],[5,6,3],[2,6,1],[4,5,6],[5,3,4],[1,2,3],[4,0,7],[7,5,6],[3,4,5],[5,2,0],[6,1,0],[6,0,4],[1,3,4],[0,2,7],[2,7,4],[7,5,6],[7,3,6],[0,4,3],[5,6,7],[5,0,7],[1,5,3],[5,1,2],[1,0,5],[3,6,7],[1,4,5],[2,5,1],[0,5,4],[6,3,0],[7,0,1],[1,5,2],[0,2,7],[6,4,2],[4,0,1],[6,1,2],[4,0,2],[1,2,4],[1,2,5],[5,3,2],[7,6,4],[1,6,0],[7,1,4],[3,1,7],[2,5,3],[5,4,1],[1,6,4],[6,3,1],[6,3,5],[5,4,2],[5,2,6],[1,6,4],[3,1,7],[0,1,3],[3,0,7],[7,5,1],[3,4,5],[2,1,6],[2,7,0],[2,4,0],[3,6,1],[1,0,3],[5,0,3],[3,6,5],[7,3,1],[5,6,1],[4,1,5],[3,0,6],[1,2,7],[3,6,1],[5,7,1],[5,6,0],[2,4,6],[1,7,4],[0,4,7],[1,2,5],[2,5,3],[7,4,5],[0,1,6],[0,6,2],[7,0,4],[7,3,1],[3,6,5],[5,3,2],[7,3,4],[6,3,0],[1,4,0],[2,3,5],[6,1,3],[2,1,6],[0,7,5],[7,5,1],[7,1,0],[4,6,3],[4,6,7],[3,4,5],[0,6,4],[5,7,0],[2,4,5],[3,7,1],[0,5,3],[5,7,4],[6,2,5],[6,5,0],[6,2,5],[0,1,7],[1,2,0]],[[0,3,5],[5,0,1],[4,7,1],[4,2,1],[6,5,4],[2,6,1],[5,4,3],[7,4,0],[7,1,4],[1,5,0],[3,1,7],[7,0,5],[7,2,1],[0,1,5],[4,5,3],[4,6,2],[4,1,3],[0,6,1],[1,7,4],[1,7,3],[1,6,0],[6,7,3],[2,5,7],[4,6,3],[4,3,1],[2,0,3],[1,3,6],[5,3,7],[7,5,2],[7,5,1],[4,1,3],[1,2,5],[5,4,6],[5,0,3],[4,5,6],[4,3,6],[0,2,7],[4,3,1],[4,5,2],[2,3,5],[7,3,5],[1,3,5],[4,1,0],[5,7,3],[6,7,5],[2,4,5],[1,3,0],[2,1,6],[0,1,3],[6,4,0],[5,2,6],[2,4,0],[3,1,2],[2,4,7],[6,5,1],[4,3,1],[3,4,6],[1,6,7],[6,4,7],[3,4,7],[3,1,6],[6,0,7],[7,6,4],[3,2,6],[3,4,6],[7,6,1],[4,1,7],[7,2,0],[7,2,0],[0,5,1],[6,4,1],[1,6,5],[5,6,4],[4,0,6],[2,4,0],[3,4,1],[7,2,3],[2,3,4],[2,6,1],[1,3,0],[1,2,3],[3,1,4],[3,7,2],[5,7,4],[0,2,3],[7,4,3],[6,7,1],[6,7,0],[7,0,6],[3,4,0],[7,3,0],[1,2,5],[7,0,5],[1,0,5],[4,0,1],[6,0,3],[0,4,5],[6,0,7],[0,7,3],[0,5,3],[6,5,2],[5,4,1],[5,1,0],[1,0,7],[5,6,2],[0,3,7],[3,5,4],[0,2,3],[7,6,0],[7,6,5],[2,4,5],[5,7,2],[7,1,5],[4,5,6],[7,3,5],[0,7,3],[5,2,0],[7,1,6],[4,0,7],[5,6,0],[4,5,2],[0,2,6],[6,3,7],[2,1,6],[2,3,1],[6,4,1],[4,6,1],[6,1,2],[1,6,2],[4,0,7],[6,5,7],[3,5,2],[6,4,5],[5,7,6],[6,3,5],[1,2,0],[6,1,7],[5,6,1],[0,5,3],[0,7,2],[5,0,2],[0,7,3],[4,1,0],[0,5,3],[2,1,0],[3,0,7],[3,5,6],[1,7,0],[0,6,5],[7,6,5],[5,1,4],[3,4,6],[7,0,1],[5,2,1],[6,1,3],[0,6,4],[6,7,1],[1,2,5],[4,6,0],[2,6,1],[1,2,7],[1,0,5],[3,4,6],[1,4,5],[6,3,5],[2,7,5],[4,1,6],[4,2,7],[6,3,1],[4,5,1],[7,6,3],[5,0,2],[0,2,1],[0,1,7],[0,1,7],[5,0,3],[1,0,7],[1,3,7],[3,7,1],[7,0,1],[2,7,1],[1,5,6],[2,6,4],[7,1,2],[3,6,1],[4,5,2],[0,4,2],[3,6,4],[0,5,3],[7,2,6],[4,3,5],[2,4,3],[6,4,0],[0,5,1],[6,7,2],[3,2,7],[7,1,3],[1,5,2],[2,7,3],[0,1,3],[5,4,7],[5,2,1],[7,0,4],[2,7,1],[4,1,7],[5,0,2],[6,5,1],[7,6,1],[3,2,1],[2,1,5],[3,5,2],[0,7,5],[3,5,0],[0,4,2],[2,7,5],[5,0,6],[3,2,7],[5,2,3],[6,7,2],[4,7,3],[7,3,4],[2,5,3],[2,0,5],[5,3,4],[1,7,3],[7,5,3],[5,1,4],[6,2,3],[4,5,0],[2,5,0],[3,4,7],[6,1,2],[6,2,4],[7,2,1],[3,1,6],[2,7,0],[6,4,1],[5,7,2],[5,2,3],[6,0,1],[1,2,0],[7,1,0],[0,6,5],[1,4,0],[1,0,7],[2,1,0],[6,5,7],[0,1,7],[1,5,6],[6,3,4],[7,4,3],[6,7,3],[0,2,4],[2,0,4],[5,0,7],[1,3,0],[5,6,0],[6,5,1],[3,0,2],[3,4,1],[2,1,0],[1,2,4],[1,2,5],[3,0,2],[6,2,0],[6,2,0],[0,3,4],[3,7,0],[3,5,6],[4,5,0],[2,4,3],[0,4,7],[5,6,7],[3,0,4],[5,2,7],[7,1,4],[7,1,6],[6,3,5],[2,1,5],[3,2,7],[0,7,4],[1,2,3],[3,4,7],[7,3,1],[4,6,3],[2,4,6],[1,5,7],[4,7,5],[1,3,2],[3,7,6],[5,3,4],[6,1,3],[5,4,0],[6,4,5],[5,4,0],[4,5,7],[1,2,7],[3,5,0],[7,4,5],[1,5,2],[2,0,1],[4,7,3],[3,4,5],[3,5,4],[2,6,7],[2,0,4],[4,2,6],[3,4,0],[0,7,4],[6,0,7],[5,7,3],[2,0,7],[3,6,2],[6,2,0],[3,0,6],[6,2,7],[6,3,5],[0,7,5],[0,6,7],[1,7,5],[4,1,6],[1,2,0],[7,4,3],[3,5,0],[3,7,0],[0,1,2],[0,7,5],[4,7,3],[4,6,5],[3,5,1],[4,0,7],[2,5,3],[4,3,1],[1,6,5],[5,1,2],[3,6,0],[7,3,0],[6,3,4],[1,6,2],[0,6,5],[6,4,3],[3,1,5],[1,3,6],[5,6,2],[2,6,5],[5,4,1],[5,4,6],[5,2,6],[2,1,4],[5,1,7],[3,6,1],[2,6,5],[3,6,7],[0,2,3],[4,5,2],[3,6,7],[4,1,5],[1,4,3],[0,5,7],[6,3,2],[0,7,4],[6,7,2],[0,2,1],[7,2,3],[6,7,2],[3,1,6],[7,0,6],[5,1,6],[0,3,1],[1,3,6],[2,6,5],[1,5,6],[2,0,7],[2,3,1],[2,3,4],[3,2,5],[1,4,7],[0,4,1],[0,3,2],[0,1,7],[1,6,7],[5,4,7],[6,2,5],[1,4,5],[1,2,5],[5,0,1],[3,1,7],[4,1,7],[5,1,4],[5,1,7],[0,3,4],[2,3,0],[0,2,7],[3,1,7],[3,4,1],[6,5,0],[0,4,3],[2,6,4],[7,2,1],[0,3,7],[2,7,6],[5,1,0],[1,3,5],[2,6,3],[5,1,3],[6,3,4],[1,3,5],[1,3,6],[7,3,0],[0,3,7],[7,4,5],[5,6,3],[3,0,6],[6,0,1],[7,0,5],[5,6,0],[7,6,0],[0,7,3],[2,6,4],[5,0,2],[1,7,0],[6,0,7],[4,0,6],[3,4,6],[1,3,7],[3,1,7],[1,3,4],[1,0,2],[3,2,1],[4,2,1],[3,2,7],[1,5,4],[3,2,5],[2,1,4],[1,2,4],[2,4,6],[2,1,3],[0,5,6],[5,6,2],[2,7,6],[2,7,6],[1,2,0],[4,6,7],[0,1,5],[0,4,6],[4,6,0],[4,2,1],[0,2,1],[2,1,5],[7,0,2],[5,0,6],[6,2,7],[0,7,6],[0,7,6],[6,5,4],[7,6,3],[0,3,2],[1,6,3],[7,4,0],[6,0,5],[6,3,0],[4,7,6],[1,2,3],[5,7,6],[5,1,4],[1,2,7],[7,2,0],[2,3,0],[4,1,7],[7,3,2],[3,0,2],[6,0,2],[2,5,0],[0,7,1],[5,2,3],[3,0,6],[3,1,0],[0,3,5],[7,0,1],[2,0,4],[5,0,6],[1,4,5],[0,6,3],[7,0,1],[1,4,5],[6,2,3],[6,3,1],[4,0,2],[7,6,3],[7,4,1],[7,0,2],[3,6,7],[0,3,2],[3,6,2],[1,0,6],[0,1,4],[4,7,2],[6,3,5],[0,7,1],[3,1,2],[5,4,7],[6,0,5],[2,5,0],[3,7,2],[2,7,5],[1,0,5],[7,6,0],[6,5,0],[5,2,0],[0,6,7],[6,5,2],[2,5,3]]]
YW = 1580
def setup_inputs(rng):
    return {"x": rng.standard_normal((N, 128, T), dtype=np.float32).astype(ml_dtypes.bfloat16)}
def reference(x):
    y = np.full((N, 128, YW), np.nan, x.dtype)
    fill = [0] * N
    for r in range(N):
        for t in range(T):
            for e in ROUTE[r][t]:
                y[e][:, fill[e]] = x[r][:, t]
                fill[e] += 1
    return {"y": y}

@@ -1,0 +1,72 @@
+N_RANKS = 8
+
+SCRATCH = {
+    "xs": ("sbuf", [128, 512], "bfloat16"),
+    "pack": ("sbuf", [128, 1536], "bfloat16"),
+    "land": ("sbuf", [128, 1580], "bfloat16"),
+}
+SEMAPHORES = ["loaded", "arrived", "sent", "stored"] + ["pk%d" % k for k in range(N_RANKS)]
+
+
+def token_runs(route_r, e):
+    runs = []
+    for t, experts in enumerate(route_r):
+        if e in experts:
+            if runs and runs[-1][1] == t:
+                runs[-1][1] = t + 1
+            else:
+                runs.append([t, t + 1])
+    return runs
+
+
+def rank_program(g, core, T, topo):
+    rank = T.rank_of(core)
+    if rank is None:
+        return
+    route = T.tables["ROUTE"]
+    n = len(T.cores)
+
+    count = [[sum(1 for ex in route[r] if e in ex) for e in range(n)] for r in range(n)]
+
+    def start(e, r):
+        return sum(count[q][e] for q in range(r))
+
+    g.sync.dma_start(T.xs[:], T.x[:]).then_inc(T.sem.loaded, 16)
+    g.sync.wait_ge(T.sem.loaded, 16)
+    g.scalar.wait_ge(T.sem.loaded, 16)
+
+    queues = (g.sync, g.scalar)
+    turn = 0
+    base = 0
+    for k in list(range(1, n)) + [0]:
+        e = (rank + k) % n
+        if k == 0:
+            buf, col = T.land, start(rank, rank)
+        else:
+            buf, col = T.pack, base
+        runs = token_runs(route[rank], e)
+        for a, b in runs:
+            queues[turn].dma_start(buf[:, col:col + (b - a)], T.xs[:, a:b]).then_inc(T.sem["pk%d" % k], 16)
+            turn = 1 - turn
+            col += b - a
+        g.wait_ge(T.sem["pk%d" % k], 16 * len(runs))
+        if k != 0:
+            dst = T.cores[e]
+            rid, pid, _se = topo.addr(dst)
+            at = start(e, rank)
+            g.remote_dma(
+                T.land[:, at:at + count[rank][e]],
+                T.pack[:, base:base + count[rank][e]],
+                T.sem.arrived,
+                T.sem.sent,
+                pid,
+                rid,
+                topo.mask(core, dst),
+            )
+            base += count[rank][e]
+
+    g.wait_ge(T.sem.arrived, 16 * (n - 1))
+    total = start(rank, n)
+    g.dma_start(T.y[:, 0:total], T.land[:, 0:total]).then_inc(T.sem.stored, 16)
+    g.wait_ge(T.sem.sent, 16 * (n - 1))
+    g.wait_ge(T.sem.stored, 16)

@@ -5,7 +5,8 @@ SCRATCH = {
     "pack": ("sbuf", [128, 1536], "bfloat16"),
     "land": ("sbuf", [128, 1580], "bfloat16"),
 }
-SEMAPHORES = ["loaded", "arrived", "sent", "stored"] + ["pk%d" % k for k in range(N_RANKS)]
+SEMAPHORES = (["loaded", "arrived", "sent", "stored"]
+              + ["pk%d" % k for k in range(N_RANKS)] + ["gk%d" % k for k in range(N_RANKS)])
 
 
 def token_runs(route_r, e):
@@ -17,6 +18,31 @@ def token_runs(route_r, e):
             else:
                 runs.append([t, t + 1])
     return runs
+
+
+def token_groups(points):
+    left = list(points)
+    groups = []
+    while len(left) > 1:
+        have = set(left)
+        best = None
+        for i, (s, p) in enumerate(left):
+            for s2, p2 in left[i + 1:]:
+                ds, dp = s2 - s, p2 - p
+                if (s - ds, p - dp) in have:
+                    continue
+                n = 2
+                while (s + n * ds, p + n * dp) in have:
+                    n += 1
+                if best is None or n > best[0]:
+                    best = (n, s, p, ds, dp)
+        groups.append(best)
+        n, s, p, ds, dp = best
+        gone = set((s + i * ds, p + i * dp) for i in range(n))
+        left = [q for q in left if q not in gone]
+    for s, p in left:
+        groups.append((1, s, p, 1, 1))
+    return groups
 
 
 def rank_program(g, core, T, topo):
@@ -31,39 +57,62 @@ def rank_program(g, core, T, topo):
     def start(e, r):
         return sum(count[q][e] for q in range(r))
 
-    g.sync.dma_start(T.xs[:], T.x[:]).then_inc(T.sem.loaded, 16)
-    g.sync.wait_ge(T.sem.loaded, 16)
-    g.scalar.wait_ge(T.sem.loaded, 16)
-
-    queues = (g.sync, g.scalar)
-    turn = 0
+    blocks = []
     base = 0
     for k in list(range(1, n)) + [0]:
         e = (rank + k) % n
         if k == 0:
-            buf, col = T.land, start(rank, rank)
+            buf, first = T.land, start(rank, rank)
         else:
-            buf, col = T.pack, base
-        runs = token_runs(route[rank], e)
-        for a, b in runs:
+            buf, first = T.pack, base
+            base += count[rank][e]
+        plain, lone, col = [], [], first
+        for a, b in token_runs(route[rank], e):
+            if b - a == 1:
+                lone.append((a, col))
+            else:
+                plain.append((a, b, col))
+            col += b - a
+        blocks.append((k, e, buf, first, plain, token_groups(lone)))
+
+    g.sync.dma_start(T.xs[:], T.x[:]).then_inc(T.sem.loaded, 16)
+    g.sync.wait_ge(T.sem.loaded, 16)
+    g.scalar.wait_ge(T.sem.loaded, 16)
+    g.wait_ge(T.sem.loaded, 16)
+
+    queues = (g.sync, g.scalar)
+    turn = 0
+    for k, e, buf, first, plain, groups in blocks:
+        for a, b, col in plain:
             queues[turn].dma_start(buf[:, col:col + (b - a)], T.xs[:, a:b]).then_inc(T.sem["pk%d" % k], 16)
             turn = 1 - turn
-            col += b - a
-        g.wait_ge(T.sem["pk%d" % k], 16 * len(runs))
+
+    for k, e, buf, first, plain, groups in blocks:
+        for m, s, p, ds, dp in groups:
+            g.dma_start(
+                buf[:, p:p + (m - 1) * dp + 1:dp],
+                T.xs[:, s:s + (m - 1) * ds + 1:ds],
+                allow_slow_non_contiguous=(m > 1),
+            ).then_inc(T.sem["gk%d" % k], 16)
+
+    for k, e, buf, first, plain, groups in blocks:
+        if plain:
+            g.wait_ge(T.sem["pk%d" % k], 16 * len(plain))
+        if groups:
+            g.wait_ge(T.sem["gk%d" % k], 16 * len(groups))
         if k != 0:
             dst = T.cores[e]
             rid, pid, _se = topo.addr(dst)
             at = start(e, rank)
             g.remote_dma(
                 T.land[:, at:at + count[rank][e]],
-                T.pack[:, base:base + count[rank][e]],
+                T.pack[:, first:first + count[rank][e]],
                 T.sem.arrived,
                 T.sem.sent,
                 pid,
                 rid,
                 topo.mask(core, dst),
             )
-            base += count[rank][e]
 
     g.wait_ge(T.sem.arrived, 16 * (n - 1))
     total = start(rank, n)

N_RANKS = 8

SCRATCH = {
    "xs": ("sbuf", [128, 512], "bfloat16"),
    "pack": ("sbuf", [128, 1536], "bfloat16"),
    "land": ("sbuf", [128, 1580], "bfloat16"),
}
SEMAPHORES = (["loaded", "arrived", "sent", "stored"]
              + ["pk%d" % k for k in range(N_RANKS)] + ["gk%d" % k for k in range(N_RANKS)])


def token_runs(route_r, e):
    runs = []
    for t, experts in enumerate(route_r):
        if e in experts:
            if runs and runs[-1][1] == t:
                runs[-1][1] = t + 1
            else:
                runs.append([t, t + 1])
    return runs


def token_groups(points):
    left = list(points)
    groups = []
    while len(left) > 1:
        have = set(left)
        best = None
        for i, (s, p) in enumerate(left):
            for s2, p2 in left[i + 1:]:
                ds, dp = s2 - s, p2 - p
                if (s - ds, p - dp) in have:
                    continue
                n = 2
                while (s + n * ds, p + n * dp) in have:
                    n += 1
                if best is None or n > best[0]:
                    best = (n, s, p, ds, dp)
        groups.append(best)
        n, s, p, ds, dp = best
        gone = set((s + i * ds, p + i * dp) for i in range(n))
        left = [q for q in left if q not in gone]
    for s, p in left:
        groups.append((1, s, p, 1, 1))
    return groups


def rank_program(g, core, T, topo):
    rank = T.rank_of(core)
    if rank is None:
        return
    route = T.tables["ROUTE"]
    n = len(T.cores)

    count = [[sum(1 for ex in route[r] if e in ex) for e in range(n)] for r in range(n)]

    def start(e, r):
        return sum(count[q][e] for q in range(r))

    blocks = []
    base = 0
    for k in list(range(1, n)) + [0]:
        e = (rank + k) % n
        if k == 0:
            buf, first = T.land, start(rank, rank)
        else:
            buf, first = T.pack, base
            base += count[rank][e]
        plain, lone, col = [], [], first
        for a, b in token_runs(route[rank], e):
            if b - a == 1:
                lone.append((a, col))
            else:
                plain.append((a, b, col))
            col += b - a
        blocks.append((k, e, buf, first, plain, token_groups(lone)))

    g.sync.dma_start(T.xs[:], T.x[:]).then_inc(T.sem.loaded, 16)
    g.sync.wait_ge(T.sem.loaded, 16)
    g.scalar.wait_ge(T.sem.loaded, 16)
    g.wait_ge(T.sem.loaded, 16)

    queues = (g.sync, g.scalar)
    turn = 0
    for k, e, buf, first, plain, groups in blocks:
        for a, b, col in plain:
            queues[turn].dma_start(buf[:, col:col + (b - a)], T.xs[:, a:b]).then_inc(T.sem["pk%d" % k], 16)
            turn = 1 - turn

    for k, e, buf, first, plain, groups in blocks:
        for m, s, p, ds, dp in groups:
            g.dma_start(
                buf[:, p:p + (m - 1) * dp + 1:dp],
                T.xs[:, s:s + (m - 1) * ds + 1:ds],
                allow_slow_non_contiguous=(m > 1),
            ).then_inc(T.sem["gk%d" % k], 16)

    for k, e, buf, first, plain, groups in blocks:
        if plain:
            g.wait_ge(T.sem["pk%d" % k], 16 * len(plain))
        if groups:
            g.wait_ge(T.sem["gk%d" % k], 16 * len(groups))
        if k != 0:
            dst = T.cores[e]
            rid, pid, _se = topo.addr(dst)
            at = start(e, rank)
            g.remote_dma(
                T.land[:, at:at + count[rank][e]],
                T.pack[:, first:first + count[rank][e]],
                T.sem.arrived,
                T.sem.sent,
                pid,
                rid,
                topo.mask(core, dst),
            )

    g.wait_ge(T.sem.arrived, 16 * (n - 1))
    total = start(rank, n)
    g.dma_start(T.y[:, 0:total], T.land[:, 0:total]).then_inc(T.sem.stored, 16)
    g.wait_ge(T.sem.sent, 16 * (n - 1))
    g.wait_ge(T.sem.stored, 16)
